import numpy as np
import ml_dtypes


def mxq(x, axis, fmt="e4m3"):
    dtype, down = {"e4m3": (ml_dtypes.float8_e4m3fn, 7), "e5m2": (ml_dtypes.float8_e5m2, 14)}[fmt]
    v = np.moveaxis(np.asarray(x, np.float32).astype(ml_dtypes.bfloat16).astype(np.float64), axis, -1)
    blocks = v.reshape(v.shape[:-1] + (-1, 32))
    amax = np.abs(blocks).max(-1, keepdims=True)
    byte = np.maximum(np.where(amax > 0, np.frexp(amax)[1] - 1 + 127, 0) - down, 1)
    scale = np.exp2(byte - 127.0)
    codes = (blocks / scale).astype(np.float32).astype(dtype).astype(np.float64)
    return np.moveaxis((codes * scale).reshape(v.shape), -1, axis)


WIDE = False


def mx_kscale(k):
    if not WIDE:
        return np.ones(k)
    levels = np.array([10, -10, 5, -5, 0])
    if k % 512:
        return np.exp2(np.random.permutation(np.resize(levels, k // 32))).repeat(32)
    a = np.empty((k // 512, 16))
    for p in range(k // 512):
        a[p, :8] = np.random.permutation(np.resize(levels, 8))
        for g in range(8):
            far = levels[np.abs(levels - a[p, g]) >= 10]
            a[p, g + 8] = far[np.random.randint(len(far))]
    return np.exp2(a.ravel()).repeat(32)


def f64(x):
    return np.asarray(x).astype(np.float64)


def striped(idx):
    return np.tile(idx.reshape(-1, 16).T, (8, 1)).astype(np.uint16)


def unstriped(offs):
    return offs[:16].T.reshape(-1).astype(np.int64)


def pack_weight(w):
    k, n = w.shape
    w = f64(np.asarray(w, np.float32).astype(ml_dtypes.bfloat16)).reshape(k // 32, 32, n)
    amax = np.abs(w).max(1)
    byte = np.clip(np.where(amax > 0, np.frexp(amax)[1] - 1 + 127 - 7, 1), 1, 254)
    scaled = (w * np.exp2(127.0 - byte)[:, None, :]).reshape(k, n).astype(np.float32)
    words = np.ascontiguousarray(scaled.reshape(k // 512, 128, 4, n).transpose(0, 1, 3, 2)).astype(ml_dtypes.float8_e4m3fn).view(np.uint8)
    return words, np.ascontiguousarray(byte.astype(np.uint8).reshape(k // 512, 16, n))


def unpack_weight(words, scales):
    g, p, n, _ = words.shape
    vals = np.ascontiguousarray(words).view(ml_dtypes.float8_e4m3fn).astype(np.float64) * np.repeat(np.exp2(scales.astype(np.float64) - 127.0), 8, axis=1)[..., None]
    return vals.transpose(0, 1, 3, 2).reshape(g * 512, n)


def relu(v):
    return np.maximum(v, 0.0)


K, T, S, D, H, N, V = 512, 1024, 512, 4, 512, 128, 128


def setup_inputs():
    n = np.random.standard_normal
    s = mx_kscale(K)[:, None]
    u = mx_kscale(H)
    packed_xT = pack_weight(n((K, T)) * s)
    return {
        "x_words": packed_xT[0],
        "x_scales": packed_xT[1],
        "w1": (n((K, H)) / np.sqrt(K) / s * u).astype(np.float32),
        "w2": (n((H, N)) / np.sqrt(H) / u[:, None]).astype(np.float32),
        "w3": (n((K, N)) / np.sqrt(K) / s).astype(np.float32),
        "known": (0.3 * n((N, V))).astype(np.float32),
        "offs": striped(np.random.permutation(T)[:S]),
    }


def reference(x_words, x_scales, w1, w2, w3, known, offs):
    xq = unpack_weight(x_words, x_scales)[:, unstriped(offs)]
    h = relu(mxq(f64(w1), 0, "e4m3").T @ xq)
    hf = mxq(f64(w2), 0, "e4m3").T @ mxq(h, 0, "e4m3")
    mh = hf.reshape(len(hf), -1, D).mean(axis=2)
    y = mxq(f64(w3), 0, "e4m3").T @ xq
    hl = hf * y
    ml = y.reshape(len(y), -1, D).mean(axis=2)
    co = hl.reshape(len(hl), -1, D).mean(axis=2) - (mh * ml)
    l2 = (y) ** 2
    va = l2.reshape(len(l2), -1, D).mean(axis=2) - ((ml) ** 2) + 0.1
    return mh + (co / va) * (f64(known) - ml)

@@ -1,0 +1,159 @@
+from contextlib import ExitStack
+
+import concourse.mybir as mybir
+
+K, T, S, D, H, N, V = 512, 1024, 512, 4, 512, 128, 128
+FLOPS = 2 * K * H * S + 2 * H * N * S + 2 * K * N * S
+
+F32 = mybir.dt.float32
+BF16 = mybir.dt.bfloat16
+I32 = mybir.dt.int32
+U32 = mybir.dt.uint32
+U16 = mybir.dt.uint16
+U8 = mybir.dt.uint8
+FP8X4 = mybir.dt.float8_e4m3fn_x4
+ALU = mybir.AluOpType
+ACT = mybir.ActivationFunctionType
+AX = mybir.AxisListType
+
+P = 128
+PACK = 4
+BLK = 128
+NB = S // BLK
+HALF = H // 2
+MH = HALF // PACK
+
+
+def tile_picked_ycvar_est_p_kernel(tc, x_words, x_scales, w1, w2, w3, known, offs, out):
+    nc = tc.nc
+    with ExitStack() as ctx:
+        sb = ctx.enter_context(tc.tile_pool(name="sb", bufs=1))
+        ps = ctx.enter_context(tc.psum_pool(name="ps", bufs=1))
+        offsets = sb.tile([P, S // 16], U16, name="offsets")
+        xw = sb.tile([P, T], U32, name="xw", align_bytes=64)
+        xs = sb.tile([P, T], U8, name="xs", align_bytes=64)
+        w3_raw = sb.tile([P, PACK, N], F32, name="w3_raw", align_bytes=64)
+        w2_raw = sb.tile([P, PACK, N], F32, name="w2_raw", align_bytes=64)
+        w1_raw = [sb.tile([P, PACK, HALF], F32, name="w1_raw%d" % u, align_bytes=64) for u in range(2)]
+        kn = sb.tile([P, V], F32, name="kn", align_bytes=64)
+        nc.vector.memset(xs[:].bitcast(I32), 0)
+        warm = sb.tile([P, 1], F32, name="warm")
+        warm2 = sb.tile([P, 1], F32, name="warm2")
+        nc.gpsimd.memset(warm[:], 1.0)
+        nc.scalar.activation(warm2[:], warm[:], ACT.Abs_reciprocal_sqrt)
+        w1_rows = w1.rearrange("(p j) c -> p j c", j=PACK)
+        nc.sync.dma_start(offsets[:], offs)
+        nc.sync.dma_start(out=w3_raw[:], in_=w3.rearrange("(p j) n -> p j n", j=PACK))
+        nc.sync.dma_start(out=kn[:], in_=known)
+        for q in range(4):
+            nc.sync.dma_start(out=xs[32 * q : 32 * q + 4, :].bitcast(I32), in_=x_scales[0, 4 * q : 4 * q + 4, :].bitcast(I32))
+        nc.sync.dma_start(out=xw[:].bitcast(I32), in_=x_words[0].rearrange("p n t -> p (n t)").bitcast(I32))
+        nc.sync.dma_start(out=w1_raw[0][:], in_=w1_rows[:, :, 0:HALF])
+        nc.sync.dma_start(out=w1_raw[1][:], in_=w1_rows[:, :, HALF:H])
+        nc.sync.dma_start(out=w2_raw[:], in_=w2.rearrange("(p j) n -> p j n", j=PACK))
+
+        def gp_cast(dst, src):
+            nc.gpsimd.tensor_scalar(dst, src, 1.0, 0.0, ALU.mult, ALU.add)
+
+        def interleave(copy, raw, name):
+            grouped = sb.tile([P, N, PACK], BF16, name=name, align_bytes=64)
+            copy(grouped[:].rearrange("p (c i) j -> p c j i", i=4), raw[:].rearrange("p j (c i) -> p c j i", i=4))
+            return grouped
+
+        def quantize(grouped, width, name):
+            codes = sb.tile([P, width], U32, name=name + "_codes", align_bytes=64)
+            scales = sb.tile([P, width], U8, name=name + "_scales", align_bytes=64)
+            nc.vector.quantize_mx(out=codes[:].bitcast(FP8X4), scales=scales[:], in_=grouped)
+            return codes, scales
+
+        def mx(acc, lhs, lcols, rhs, rcols):
+            nc.tensor.matmul_mx(out=acc, lhsT=lhs[0][:, lcols].bitcast(FP8X4), lhsT_scale=lhs[1][:, lcols], rhs=rhs[0][:, rcols].bitcast(FP8X4), rhs_scale=rhs[1][:, rcols], start=True, stop=True)
+
+        w1_g = sb.tile([P, PACK, P, PACK], BF16, name="w1_g", align_bytes=64)
+
+        def deal_w1(copy, u, m0, m1):
+            dst = w1_g[:, :, u * MH + m0 : u * MH + m1, :].rearrange("p t m j -> p m j t")
+            src = w1_raw[u][:, :, PACK * m0 : PACK * m1].rearrange("p j (m t) -> p m j t", t=PACK)
+            copy(dst, src)
+
+        gs = sb.tile([P, S], U8, name="gs", align_bytes=64)
+        gw = sb.tile([P, S], U32, name="gw", align_bytes=64)
+        xq = (gw, gs)
+        full = slice(0, P)
+        y = [ps.tile([P, S // 2], F32, name="y%d" % u) for u in range(2)]
+        y3 = [y[u][:].rearrange("p (v d) -> p v d", d=D) for u in range(2)]
+        sy = sb.tile([P, V], F32, name="sy")
+        yc = sb.tile([P, V, D], F32, name="yc")
+        halves = [slice(u * V // 2, (u + 1) * V // 2) for u in range(2)]
+        sq = w1_raw[1][:].rearrange("p j c -> p (j c)")[:, 0:S].rearrange("p (v d) -> p v d", d=D)
+        svv = sb.tile([P, V], F32, name="svv")
+        kneg = sb.tile([P, V], F32, name="kneg")
+        rs = sb.tile([P, V], F32, name="rs")
+        r0 = sb.tile([P, V], F32, name="r0")
+        e = sb.tile([P, V], F32, name="e")
+        g0 = sb.tile([P, V], F32, name="g0")
+        g = sb.tile([P, V], F32, name="g")
+        c = sb.tile([P, V, D], F32, name="c")
+        c2 = c[:].rearrange("p v d -> p (v d)")
+        res = sb.tile([P, V], F32, name="res")
+        h_ps = [ps.tile([P, PACK, BLK], F32, name="h_ps%d" % b) for b in range(NB)]
+        h_g = sb.tile([P, S, PACK], BF16, name="h_g", align_bytes=64)
+        h_q = {}
+        prods = {}
+        w1_q = []
+
+        nc.vector.tensor_copy(gs[:], xs[:].indirect(offsets[:]))
+        w3_g = interleave(nc.scalar.copy, w3_raw, "w3_g")
+        w3_q = quantize(w3_g[:].rearrange("p c j -> p (c j)"), N, "w3")
+        nc.vector.tensor_copy(gw[:, 0 * 256 : 0 * 256 + 256], xw[:].indirect(offsets[:, 0 * 16 : 0 * 16 + 16]))
+        mx(y[0][:], w3_q, full, xq, slice(0 * 256, 0 * 256 + 256))
+        nc.vector.tensor_copy(gw[:, 1 * 256 : 1 * 256 + 256], xw[:].indirect(offsets[:, 1 * 16 : 1 * 16 + 16]))
+        mx(y[1][:], w3_q, full, xq, slice(1 * 256, 1 * 256 + 256))
+        deal_w1(nc.scalar.copy, 0, 0, 64)
+        nc.vector.tensor_reduce(sy[:, halves[0]], y3[0], AX.X, ALU.add)
+        nc.vector.tensor_reduce(sy[:, halves[1]], y3[1], AX.X, ALU.add)
+        nc.vector.scalar_tensor_tensor(yc[:, halves[0], :], sy[:, halves[0]].unsqueeze(2).to_broadcast([P, V // 2, D]), -1.0 / D, y3[0], ALU.mult, ALU.add)
+        nc.vector.scalar_tensor_tensor(yc[:, halves[1], :], sy[:, halves[1]].unsqueeze(2).to_broadcast([P, V // 2, D]), -1.0 / D, y3[1], ALU.mult, ALU.add)
+        deal_w1(nc.scalar.copy, 1, 0, 44)
+        deal_w1(nc.vector.tensor_copy, 1, 44, 64)
+        for k in range(2):
+            w1_q.append(quantize(w1_g[:, k * 2 : (k + 1) * 2].rearrange("p t m j -> p (t m j)"), P * 2, "w1_%d" % k))
+        for b in range(NB):
+            for t in range(PACK):
+                mx(h_ps[b][:, t, :], w1_q[t // 2], slice((t % 2) * P, (t % 2 + 1) * P), xq, slice(b * BLK, (b + 1) * BLK))
+        nc.scalar.activation(sq, yc[:], ACT.Square)
+        w2_g = interleave(nc.scalar.copy, w2_raw, "w2_g")
+        nc.vector.tensor_reduce(svv[:], sq, AX.X, ALU.add)
+        nc.vector.scalar_tensor_tensor(kneg[:], sy[:], 1.0 / D, kn[:], ALU.mult, ALU.subtract)
+        w2_q = quantize(w2_g[:].rearrange("p c j -> p (c j)"), N, "w2")
+        nc.scalar.activation(h_g[:, 0 * BLK : 0 * BLK + BLK, :], h_ps[0][:].rearrange("p t j -> p j t"), ACT.Relu)
+        nc.scalar.activation(rs[:], svv[:], ACT.Abs_reciprocal_sqrt, bias=0.1 * D)
+        nc.scalar.activation(r0[:], rs[:], ACT.Square)
+        nc.scalar.activation(h_g[:, 1 * BLK : 1 * BLK + BLK, :], h_ps[1][:].rearrange("p t j -> p j t"), ACT.Relu)
+        nc.scalar.activation(h_g[:, 2 * BLK : 2 * BLK + BLK, :], h_ps[2][:].rearrange("p t j -> p j t"), ACT.Relu)
+        nc.scalar.activation(h_g[:, 3 * BLK : 3 * BLK + BLK, :], h_ps[3][:].rearrange("p t j -> p j t"), ACT.Relu)
+        nc.vector.scalar_tensor_tensor(e[:], svv[:], 0.1 * D, r0[:], ALU.add, ALU.mult)
+        nc.vector.tensor_tensor(g0[:], kneg[:], r0[:], ALU.mult)
+        h_q[0] = quantize(h_g[:, 0 * BLK : 1 * BLK, :].rearrange("p j t -> p (j t)"), 1 * BLK, "h0")
+        nc.vector.scalar_tensor_tensor(g[:], e[:], 2.0, g0[:], ALU.subtract, ALU.mult)
+        h_q[1] = quantize(h_g[:, 1 * BLK : 2 * BLK, :].rearrange("p j t -> p (j t)"), 1 * BLK, "h1")
+        nc.vector.tensor_tensor(c[:, 0:128, :], yc[:, 0:128, :], g[:, 0:128].unsqueeze(2).to_broadcast([P, 128, D]), ALU.mult)
+        h_q[2] = quantize(h_g[:, 2 * BLK : 3 * BLK, :].rearrange("p j t -> p (j t)"), 1 * BLK, "h2")
+        h_q[3] = quantize(h_g[:, 3 * BLK : 4 * BLK, :].rearrange("p j t -> p (j t)"), 1 * BLK, "h3")
+        hf0 = ps.tile([P, 2 * BLK], F32, name="hf0", tag="hfa")
+        mx(hf0[:, 0 * BLK : 1 * BLK], w2_q, full, h_q[0], slice(0, 1 * BLK))
+        mx(hf0[:, 1 * BLK : 2 * BLK], w2_q, full, h_q[1], slice(0, 1 * BLK))
+        hf2 = ps.tile([P, 1 * BLK], F32, name="hf2", tag="hfb")
+        mx(hf2[:, 0 * BLK : 1 * BLK], w2_q, full, h_q[2], slice(0, 1 * BLK))
+        hf3 = ps.tile([P, 1 * BLK], F32, name="hf3", tag="h_ps0")
+        mx(hf3[:, 0 * BLK : 1 * BLK], w2_q, full, h_q[3], slice(0, 1 * BLK))
+        prods[0] = sb.tile([P, 2 * BLK], F32, name="prod0")
+        nc.vector.scalar_tensor_tensor(prods[0][:], c2[:, 0 * BLK : 2 * BLK], 1.0 / D, hf0[:], ALU.add, ALU.mult)
+        prods[2] = sb.tile([P, 1 * BLK], F32, name="prod2")
+        nc.vector.scalar_tensor_tensor(prods[2][:], c2[:, 2 * BLK : 3 * BLK], 1.0 / D, hf2[:], ALU.add, ALU.mult)
+        nc.vector.tensor_reduce(res[:, 0 * 32 : 2 * 32], prods[0][:].rearrange("p (v d) -> p v d", d=D), AX.X, ALU.add)
+        prods[3] = sb.tile([P, 1 * BLK], F32, name="prod3")
+        nc.vector.scalar_tensor_tensor(prods[3][:], c2[:, 3 * BLK : 4 * BLK], 1.0 / D, hf3[:], ALU.add, ALU.mult)
+        nc.vector.tensor_reduce(res[:, 2 * 32 : 3 * 32], prods[2][:].rearrange("p (v d) -> p v d", d=D), AX.X, ALU.add)
+        nc.vector.tensor_reduce(res[:, 3 * 32 : 4 * 32], prods[3][:].rearrange("p (v d) -> p v d", d=D), AX.X, ALU.add)
+        nc.sync.dma_start(out=out[:, 0:128], in_=res[:, 0:128])

@@ -44,13 +44,13 @@ def tile_picked_ycvar_est_p_kernel(tc, x_words, x_scales, w1, w2, w3, known, off
         w1_rows = w1.rearrange("(p j) c -> p j c", j=PACK)
         nc.sync.dma_start(offsets[:], offs)
         nc.sync.dma_start(out=w3_raw[:], in_=w3.rearrange("(p j) n -> p j n", j=PACK))
-        nc.sync.dma_start(out=kn[:], in_=known)
         for q in range(4):
             nc.sync.dma_start(out=xs[32 * q : 32 * q + 4, :].bitcast(I32), in_=x_scales[0, 4 * q : 4 * q + 4, :].bitcast(I32))
         nc.sync.dma_start(out=xw[:].bitcast(I32), in_=x_words[0].rearrange("p n t -> p (n t)").bitcast(I32))
         nc.sync.dma_start(out=w1_raw[0][:], in_=w1_rows[:, :, 0:HALF])
         nc.sync.dma_start(out=w1_raw[1][:], in_=w1_rows[:, :, HALF:H])
         nc.sync.dma_start(out=w2_raw[:], in_=w2.rearrange("(p j) n -> p j n", j=PACK))
+        nc.sync.dma_start(out=kn[:], in_=known)
 
         def gp_cast(dst, src):
             nc.gpsimd.tensor_scalar(dst, src, 1.0, 0.0, ALU.mult, ALU.add)
@@ -85,10 +85,10 @@ def tile_picked_ycvar_est_p_kernel(tc, x_words, x_scales, w1, w2, w3, known, off
         sy = sb.tile([P, V], F32, name="sy")
         yc = sb.tile([P, V, D], F32, name="yc")
         halves = [slice(u * V // 2, (u + 1) * V // 2) for u in range(2)]
-        sq = w1_raw[1][:].rearrange("p j c -> p (j c)")[:, 0:S].rearrange("p (v d) -> p v d", d=D)
+        sq = w1_raw[0][:].rearrange("p j c -> p (j c)")[:, 0:S].rearrange("p (v d) -> p v d", d=D)
         svv = sb.tile([P, V], F32, name="svv")
         kneg = sb.tile([P, V], F32, name="kneg")
-        rs = sb.tile([P, V], F32, name="rs")
+        rs = sb.tile([P, V], F32, name="rs", tag="rs", align_bytes=64)
         r0 = sb.tile([P, V], F32, name="r0")
         e = sb.tile([P, V], F32, name="e")
         g0 = sb.tile([P, V], F32, name="g0")
@@ -97,7 +97,7 @@ def tile_picked_ycvar_est_p_kernel(tc, x_words, x_scales, w1, w2, w3, known, off
         c2 = c[:].rearrange("p v d -> p (v d)")
         res = sb.tile([P, V], F32, name="res")
         h_ps = [ps.tile([P, PACK, BLK], F32, name="h_ps%d" % b) for b in range(NB)]
-        h_g = sb.tile([P, S, PACK], BF16, name="h_g", align_bytes=64)
+        h_g = {}
         h_q = {}
         prods = {}
         w1_q = []
@@ -107,53 +107,53 @@ def tile_picked_ycvar_est_p_kernel(tc, x_words, x_scales, w1, w2, w3, known, off
         w3_q = quantize(w3_g[:].rearrange("p c j -> p (c j)"), N, "w3")
         nc.vector.tensor_copy(gw[:, 0 * 256 : 0 * 256 + 256], xw[:].indirect(offsets[:, 0 * 16 : 0 * 16 + 16]))
         mx(y[0][:], w3_q, full, xq, slice(0 * 256, 0 * 256 + 256))
+        mx(h_ps[3][:].rearrange("p t j -> p (t j)")[:, 0:256], w3_q, full, xq, slice(0, 256))
         nc.vector.tensor_copy(gw[:, 1 * 256 : 1 * 256 + 256], xw[:].indirect(offsets[:, 1 * 16 : 1 * 16 + 16]))
         mx(y[1][:], w3_q, full, xq, slice(1 * 256, 1 * 256 + 256))
+        mx(h_ps[3][:].rearrange("p t j -> p (t j)")[:, 0:512], w3_q, full, xq, slice(0, 512))
         deal_w1(nc.scalar.copy, 0, 0, 64)
         nc.vector.tensor_reduce(sy[:, halves[0]], y3[0], AX.X, ALU.add)
         nc.vector.tensor_reduce(sy[:, halves[1]], y3[1], AX.X, ALU.add)
         nc.vector.scalar_tensor_tensor(yc[:, halves[0], :], sy[:, halves[0]].unsqueeze(2).to_broadcast([P, V // 2, D]), -1.0 / D, y3[0], ALU.mult, ALU.add)
         nc.vector.scalar_tensor_tensor(yc[:, halves[1], :], sy[:, halves[1]].unsqueeze(2).to_broadcast([P, V // 2, D]), -1.0 / D, y3[1], ALU.mult, ALU.add)
-        deal_w1(nc.scalar.copy, 1, 0, 44)
-        deal_w1(nc.vector.tensor_copy, 1, 44, 64)
+        deal_w1(nc.scalar.copy, 1, 0, 64)
         for k in range(2):
             w1_q.append(quantize(w1_g[:, k * 2 : (k + 1) * 2].rearrange("p t m j -> p (t m j)"), P * 2, "w1_%d" % k))
         for b in range(NB):
             for t in range(PACK):
                 mx(h_ps[b][:, t, :], w1_q[t // 2], slice((t % 2) * P, (t % 2 + 1) * P), xq, slice(b * BLK, (b + 1) * BLK))
         nc.scalar.activation(sq, yc[:], ACT.Square)
-        w2_g = interleave(nc.scalar.copy, w2_raw, "w2_g")
+        pair0 = sb.tile([P, 2, BLK, PACK], BF16, name="pair0", align_bytes=64)
+        gp_cast(pair0[:, 0].rearrange("p (c i) j -> p c j i", i=4), w2_raw[:].rearrange("p j (c i) -> p c j i", i=4))
         nc.vector.tensor_reduce(svv[:], sq, AX.X, ALU.add)
         nc.vector.scalar_tensor_tensor(kneg[:], sy[:], 1.0 / D, kn[:], ALU.mult, ALU.subtract)
-        w2_q = quantize(w2_g[:].rearrange("p c j -> p (c j)"), N, "w2")
-        nc.scalar.activation(h_g[:, 0 * BLK : 0 * BLK + BLK, :], h_ps[0][:].rearrange("p t j -> p j t"), ACT.Relu)
+        nc.scalar.activation(pair0[:, 1], h_ps[0][:].rearrange("p t j -> p j t"), ACT.Relu)
         nc.scalar.activation(rs[:], svv[:], ACT.Abs_reciprocal_sqrt, bias=0.1 * D)
-        nc.scalar.activation(r0[:], rs[:], ACT.Square)
-        nc.scalar.activation(h_g[:, 1 * BLK : 1 * BLK + BLK, :], h_ps[1][:].rearrange("p t j -> p j t"), ACT.Relu)
-        nc.scalar.activation(h_g[:, 2 * BLK : 2 * BLK + BLK, :], h_ps[2][:].rearrange("p t j -> p j t"), ACT.Relu)
-        nc.scalar.activation(h_g[:, 3 * BLK : 3 * BLK + BLK, :], h_ps[3][:].rearrange("p t j -> p j t"), ACT.Relu)
-        nc.vector.scalar_tensor_tensor(e[:], svv[:], 0.1 * D, r0[:], ALU.add, ALU.mult)
-        nc.vector.tensor_tensor(g0[:], kneg[:], r0[:], ALU.mult)
-        h_q[0] = quantize(h_g[:, 0 * BLK : 1 * BLK, :].rearrange("p j t -> p (j t)"), 1 * BLK, "h0")
-        nc.vector.scalar_tensor_tensor(g[:], e[:], 2.0, g0[:], ALU.subtract, ALU.mult)
-        h_q[1] = quantize(h_g[:, 1 * BLK : 2 * BLK, :].rearrange("p j t -> p (j t)"), 1 * BLK, "h1")
+        h_g[1] = sb.tile([P, BLK, PACK], BF16, name="h_g1", align_bytes=64)
+        nc.scalar.activation(h_g[1][:], h_ps[1][:].rearrange("p t j -> p j t"), ACT.Relu)
+        h_g[2] = sb.tile([P, BLK, PACK], BF16, name="h_g2", align_bytes=64)
+        nc.scalar.activation(h_g[2][:], h_ps[2][:].rearrange("p t j -> p j t"), ACT.Relu)
+        h_g[3] = sb.tile([P, BLK, PACK], BF16, name="h_g3", align_bytes=64)
+        nc.scalar.activation(h_g[3][:], h_ps[3][:].rearrange("p t j -> p j t"), ACT.Relu)
+        nc.vector.scalar_tensor_tensor(g0[:], kneg[:], -1.0, rs[:], ALU.mult, ALU.mult)
+        pq0 = quantize(pair0[:].rearrange("p s j t -> p (s j t)"), 2 * BLK, "pq0")
+        hf0 = ps.tile([P, 2 * BLK], F32, name="hf0")
+        mx(hf0[:, 0:BLK], pq0, full, pq0, slice(BLK, 2 * BLK))
+        nc.vector.tensor_tensor(g[:], g0[:], rs[:], ALU.mult)
+        h_q[1] = quantize(h_g[1][:].rearrange("p j t -> p (j t)"), BLK, "h1")
+        mx(hf0[:, 1 * BLK : 2 * BLK], pq0, full, h_q[1], full)
         nc.vector.tensor_tensor(c[:, 0:128, :], yc[:, 0:128, :], g[:, 0:128].unsqueeze(2).to_broadcast([P, 128, D]), ALU.mult)
-        h_q[2] = quantize(h_g[:, 2 * BLK : 3 * BLK, :].rearrange("p j t -> p (j t)"), 1 * BLK, "h2")
-        h_q[3] = quantize(h_g[:, 3 * BLK : 4 * BLK, :].rearrange("p j t -> p (j t)"), 1 * BLK, "h3")
-        hf0 = ps.tile([P, 2 * BLK], F32, name="hf0", tag="hfa")
-        mx(hf0[:, 0 * BLK : 1 * BLK], w2_q, full, h_q[0], slice(0, 1 * BLK))
-        mx(hf0[:, 1 * BLK : 2 * BLK], w2_q, full, h_q[1], slice(0, 1 * BLK))
-        hf2 = ps.tile([P, 1 * BLK], F32, name="hf2", tag="hfb")
-        mx(hf2[:, 0 * BLK : 1 * BLK], w2_q, full, h_q[2], slice(0, 1 * BLK))
-        hf3 = ps.tile([P, 1 * BLK], F32, name="hf3", tag="h_ps0")
-        mx(hf3[:, 0 * BLK : 1 * BLK], w2_q, full, h_q[3], slice(0, 1 * BLK))
-        prods[0] = sb.tile([P, 2 * BLK], F32, name="prod0")
-        nc.vector.scalar_tensor_tensor(prods[0][:], c2[:, 0 * BLK : 2 * BLK], 1.0 / D, hf0[:], ALU.add, ALU.mult)
-        prods[2] = sb.tile([P, 1 * BLK], F32, name="prod2")
-        nc.vector.scalar_tensor_tensor(prods[2][:], c2[:, 2 * BLK : 3 * BLK], 1.0 / D, hf2[:], ALU.add, ALU.mult)
-        nc.vector.tensor_reduce(res[:, 0 * 32 : 2 * 32], prods[0][:].rearrange("p (v d) -> p v d", d=D), AX.X, ALU.add)
-        prods[3] = sb.tile([P, 1 * BLK], F32, name="prod3")
-        nc.vector.scalar_tensor_tensor(prods[3][:], c2[:, 3 * BLK : 4 * BLK], 1.0 / D, hf3[:], ALU.add, ALU.mult)
-        nc.vector.tensor_reduce(res[:, 2 * 32 : 3 * 32], prods[2][:].rearrange("p (v d) -> p v d", d=D), AX.X, ALU.add)
-        nc.vector.tensor_reduce(res[:, 3 * 32 : 4 * 32], prods[3][:].rearrange("p (v d) -> p v d", d=D), AX.X, ALU.add)
+        h_q[2] = quantize(h_g[2][:].rearrange("p j t -> p (j t)"), BLK, "h2")
+        hf2 = ps.tile([P, 1 * BLK], F32, name="hf2")
+        mx(hf2[:, 0 * BLK : 1 * BLK], pq0, full, h_q[2], full)
+        h_q[3] = quantize(h_g[3][:].rearrange("p j t -> p (j t)"), BLK, "h3")
+        hf3 = ps.tile([P, 1 * BLK], F32, name="hf3", tag="y0")
+        mx(hf3[:, 0 * BLK : 1 * BLK], pq0, full, h_q[3], full)
+        prod = sb.tile([P, S], F32, name="prod")
+        nc.vector.scalar_tensor_tensor(prod[:, 0 * BLK : 2 * BLK], c2[:, 0 * BLK : 2 * BLK], 1.0 / D, hf0[:], ALU.add, ALU.mult)
+        nc.vector.scalar_tensor_tensor(prod[:, 2 * BLK : 3 * BLK], c2[:, 2 * BLK : 3 * BLK], 1.0 / D, hf2[:], ALU.add, ALU.mult)
+        nc.vector.tensor_reduce(res[:, 0 * 32 : 2 * 32], prod[:, 0 * BLK : 2 * BLK].rearrange("p (v d) -> p v d", d=D), AX.X, ALU.add)
+        nc.vector.tensor_reduce(res[:, 2 * 32 : 3 * 32], prod[:, 2 * BLK : 3 * BLK].rearrange("p (v d) -> p v d", d=D), AX.X, ALU.add)
+        nc.vector.scalar_tensor_tensor(prod[:, 3 * BLK : 4 * BLK], c2[:, 3 * BLK : 4 * BLK], 1.0 / D, hf3[:], ALU.add, ALU.mult)
+        nc.vector.tensor_reduce(res[:, 3 * 32 : 4 * 32], prod[:, 3 * BLK : 4 * BLK].rearrange("p (v d) -> p v d", d=D), AX.X, ALU.add)
         nc.sync.dma_start(out=out[:, 0:128], in_=res[:, 0:128])

from contextlib import ExitStack

import concourse.mybir as mybir

K, T, S, D, H, N, V = 512, 1024, 512, 4, 512, 128, 128
FLOPS = 2 * K * H * S + 2 * H * N * S + 2 * K * N * S

F32 = mybir.dt.float32
BF16 = mybir.dt.bfloat16
I32 = mybir.dt.int32
U32 = mybir.dt.uint32
U16 = mybir.dt.uint16
U8 = mybir.dt.uint8
FP8X4 = mybir.dt.float8_e4m3fn_x4
ALU = mybir.AluOpType
ACT = mybir.ActivationFunctionType
AX = mybir.AxisListType

P = 128
PACK = 4
BLK = 128
NB = S // BLK
HALF = H // 2
MH = HALF // PACK


def tile_picked_ycvar_est_p_kernel(tc, x_words, x_scales, w1, w2, w3, known, offs, out):
    nc = tc.nc
    with ExitStack() as ctx:
        sb = ctx.enter_context(tc.tile_pool(name="sb", bufs=1))
        ps = ctx.enter_context(tc.psum_pool(name="ps", bufs=1))
        offsets = sb.tile([P, S // 16], U16, name="offsets")
        xw = sb.tile([P, T], U32, name="xw", align_bytes=64)
        xs = sb.tile([P, T], U8, name="xs", align_bytes=64)
        w3_raw = sb.tile([P, PACK, N], F32, name="w3_raw", align_bytes=64)
        w2_raw = sb.tile([P, PACK, N], F32, name="w2_raw", align_bytes=64)
        w1_raw = [sb.tile([P, PACK, HALF], F32, name="w1_raw%d" % u, align_bytes=64) for u in range(2)]
        kn = sb.tile([P, V], F32, name="kn", align_bytes=64)
        nc.vector.memset(xs[:].bitcast(I32), 0)
        warm = sb.tile([P, 1], F32, name="warm")
        warm2 = sb.tile([P, 1], F32, name="warm2")
        nc.gpsimd.memset(warm[:], 1.0)
        nc.scalar.activation(warm2[:], warm[:], ACT.Abs_reciprocal_sqrt)
        w1_rows = w1.rearrange("(p j) c -> p j c", j=PACK)
        nc.sync.dma_start(offsets[:], offs)
        nc.sync.dma_start(out=w3_raw[:], in_=w3.rearrange("(p j) n -> p j n", j=PACK))
        for q in range(4):
            nc.sync.dma_start(out=xs[32 * q : 32 * q + 4, :].bitcast(I32), in_=x_scales[0, 4 * q : 4 * q + 4, :].bitcast(I32))
        nc.sync.dma_start(out=xw[:].bitcast(I32), in_=x_words[0].rearrange("p n t -> p (n t)").bitcast(I32))
        nc.sync.dma_start(out=w1_raw[0][:], in_=w1_rows[:, :, 0:HALF])
        nc.sync.dma_start(out=w1_raw[1][:], in_=w1_rows[:, :, HALF:H])
        nc.sync.dma_start(out=w2_raw[:], in_=w2.rearrange("(p j) n -> p j n", j=PACK))
        nc.sync.dma_start(out=kn[:], in_=known)

        def gp_cast(dst, src):
            nc.gpsimd.tensor_scalar(dst, src, 1.0, 0.0, ALU.mult, ALU.add)

        def interleave(copy, raw, name):
            grouped = sb.tile([P, N, PACK], BF16, name=name, align_bytes=64)
            copy(grouped[:].rearrange("p (c i) j -> p c j i", i=4), raw[:].rearrange("p j (c i) -> p c j i", i=4))
            return grouped

        def quantize(grouped, width, name):
            codes = sb.tile([P, width], U32, name=name + "_codes", align_bytes=64)
            scales = sb.tile([P, width], U8, name=name + "_scales", align_bytes=64)
            nc.vector.quantize_mx(out=codes[:].bitcast(FP8X4), scales=scales[:], in_=grouped)
            return codes, scales

        def mx(acc, lhs, lcols, rhs, rcols):
            nc.tensor.matmul_mx(out=acc, lhsT=lhs[0][:, lcols].bitcast(FP8X4), lhsT_scale=lhs[1][:, lcols], rhs=rhs[0][:, rcols].bitcast(FP8X4), rhs_scale=rhs[1][:, rcols], start=True, stop=True)

        w1_g = sb.tile([P, PACK, P, PACK], BF16, name="w1_g", align_bytes=64)

        def deal_w1(copy, u, m0, m1):
            dst = w1_g[:, :, u * MH + m0 : u * MH + m1, :].rearrange("p t m j -> p m j t")
            src = w1_raw[u][:, :, PACK * m0 : PACK * m1].rearrange("p j (m t) -> p m j t", t=PACK)
            copy(dst, src)

        gs = sb.tile([P, S], U8, name="gs", align_bytes=64)
        gw = sb.tile([P, S], U32, name="gw", align_bytes=64)
        xq = (gw, gs)
        full = slice(0, P)
        y = [ps.tile([P, S // 2], F32, name="y%d" % u) for u in range(2)]
        y3 = [y[u][:].rearrange("p (v d) -> p v d", d=D) for u in range(2)]
        sy = sb.tile([P, V], F32, name="sy")
        yc = sb.tile([P, V, D], F32, name="yc")
        halves = [slice(u * V // 2, (u + 1) * V // 2) for u in range(2)]
        sq = w1_raw[0][:].rearrange("p j c -> p (j c)")[:, 0:S].rearrange("p (v d) -> p v d", d=D)
        svv = sb.tile([P, V], F32, name="svv")
        kneg = sb.tile([P, V], F32, name="kneg")
        rs = sb.tile([P, V], F32, name="rs", tag="rs", align_bytes=64)
        r0 = sb.tile([P, V], F32, name="r0")
        e = sb.tile([P, V], F32, name="e")
        g0 = sb.tile([P, V], F32, name="g0")
        g = sb.tile([P, V], F32, name="g")
        c = sb.tile([P, V, D], F32, name="c")
        c2 = c[:].rearrange("p v d -> p (v d)")
        res = sb.tile([P, V], F32, name="res")
        h_ps = [ps.tile([P, PACK, BLK], F32, name="h_ps%d" % b) for b in range(NB)]
        h_g = {}
        h_q = {}
        prods = {}
        w1_q = []

        nc.vector.tensor_copy(gs[:], xs[:].indirect(offsets[:]))
        w3_g = interleave(nc.scalar.copy, w3_raw, "w3_g")
        w3_q = quantize(w3_g[:].rearrange("p c j -> p (c j)"), N, "w3")
        nc.vector.tensor_copy(gw[:, 0 * 256 : 0 * 256 + 256], xw[:].indirect(offsets[:, 0 * 16 : 0 * 16 + 16]))
        mx(y[0][:], w3_q, full, xq, slice(0 * 256, 0 * 256 + 256))
        mx(h_ps[3][:].rearrange("p t j -> p (t j)")[:, 0:256], w3_q, full, xq, slice(0, 256))
        nc.vector.tensor_copy(gw[:, 1 * 256 : 1 * 256 + 256], xw[:].indirect(offsets[:, 1 * 16 : 1 * 16 + 16]))
        mx(y[1][:], w3_q, full, xq, slice(1 * 256, 1 * 256 + 256))
        mx(h_ps[3][:].rearrange("p t j -> p (t j)")[:, 0:512], w3_q, full, xq, slice(0, 512))
        deal_w1(nc.scalar.copy, 0, 0, 64)
        nc.vector.tensor_reduce(sy[:, halves[0]], y3[0], AX.X, ALU.add)
        nc.vector.tensor_reduce(sy[:, halves[1]], y3[1], AX.X, ALU.add)
        nc.vector.scalar_tensor_tensor(yc[:, halves[0], :], sy[:, halves[0]].unsqueeze(2).to_broadcast([P, V // 2, D]), -1.0 / D, y3[0], ALU.mult, ALU.add)
        nc.vector.scalar_tensor_tensor(yc[:, halves[1], :], sy[:, halves[1]].unsqueeze(2).to_broadcast([P, V // 2, D]), -1.0 / D, y3[1], ALU.mult, ALU.add)
        deal_w1(nc.scalar.copy, 1, 0, 64)
        for k in range(2):
            w1_q.append(quantize(w1_g[:, k * 2 : (k + 1) * 2].rearrange("p t m j -> p (t m j)"), P * 2, "w1_%d" % k))
        for b in range(NB):
            for t in range(PACK):
                mx(h_ps[b][:, t, :], w1_q[t // 2], slice((t % 2) * P, (t % 2 + 1) * P), xq, slice(b * BLK, (b + 1) * BLK))
        nc.scalar.activation(sq, yc[:], ACT.Square)
        pair0 = sb.tile([P, 2, BLK, PACK], BF16, name="pair0", align_bytes=64)
        gp_cast(pair0[:, 0].rearrange("p (c i) j -> p c j i", i=4), w2_raw[:].rearrange("p j (c i) -> p c j i", i=4))
        nc.vector.tensor_reduce(svv[:], sq, AX.X, ALU.add)
        nc.vector.scalar_tensor_tensor(kneg[:], sy[:], 1.0 / D, kn[:], ALU.mult, ALU.subtract)
        nc.scalar.activation(pair0[:, 1], h_ps[0][:].rearrange("p t j -> p j t"), ACT.Relu)
        nc.scalar.activation(rs[:], svv[:], ACT.Abs_reciprocal_sqrt, bias=0.1 * D)
        h_g[1] = sb.tile([P, BLK, PACK], BF16, name="h_g1", align_bytes=64)
        nc.scalar.activation(h_g[1][:], h_ps[1][:].rearrange("p t j -> p j t"), ACT.Relu)
        h_g[2] = sb.tile([P, BLK, PACK], BF16, name="h_g2", align_bytes=64)
        nc.scalar.activation(h_g[2][:], h_ps[2][:].rearrange("p t j -> p j t"), ACT.Relu)
        h_g[3] = sb.tile([P, BLK, PACK], BF16, name="h_g3", align_bytes=64)
        nc.scalar.activation(h_g[3][:], h_ps[3][:].rearrange("p t j -> p j t"), ACT.Relu)
        nc.vector.scalar_tensor_tensor(g0[:], kneg[:], -1.0, rs[:], ALU.mult, ALU.mult)
        pq0 = quantize(pair0[:].rearrange("p s j t -> p (s j t)"), 2 * BLK, "pq0")
        hf0 = ps.tile([P, 2 * BLK], F32, name="hf0")
        mx(hf0[:, 0:BLK], pq0, full, pq0, slice(BLK, 2 * BLK))
        nc.vector.tensor_tensor(g[:], g0[:], rs[:], ALU.mult)
        h_q[1] = quantize(h_g[1][:].rearrange("p j t -> p (j t)"), BLK, "h1")
        mx(hf0[:, 1 * BLK : 2 * BLK], pq0, full, h_q[1], full)
        nc.vector.tensor_tensor(c[:, 0:128, :], yc[:, 0:128, :], g[:, 0:128].unsqueeze(2).to_broadcast([P, 128, D]), ALU.mult)
        h_q[2] = quantize(h_g[2][:].rearrange("p j t -> p (j t)"), BLK, "h2")
        hf2 = ps.tile([P, 1 * BLK], F32, name="hf2")
        mx(hf2[:, 0 * BLK : 1 * BLK], pq0, full, h_q[2], full)
        h_q[3] = quantize(h_g[3][:].rearrange("p j t -> p (j t)"), BLK, "h3")
        hf3 = ps.tile([P, 1 * BLK], F32, name="hf3", tag="y0")
        mx(hf3[:, 0 * BLK : 1 * BLK], pq0, full, h_q[3], full)
        prod = sb.tile([P, S], F32, name="prod")
        nc.vector.scalar_tensor_tensor(prod[:, 0 * BLK : 2 * BLK], c2[:, 0 * BLK : 2 * BLK], 1.0 / D, hf0[:], ALU.add, ALU.mult)
        nc.vector.scalar_tensor_tensor(prod[:, 2 * BLK : 3 * BLK], c2[:, 2 * BLK : 3 * BLK], 1.0 / D, hf2[:], ALU.add, ALU.mult)
        nc.vector.tensor_reduce(res[:, 0 * 32 : 2 * 32], prod[:, 0 * BLK : 2 * BLK].rearrange("p (v d) -> p v d", d=D), AX.X, ALU.add)
        nc.vector.tensor_reduce(res[:, 2 * 32 : 3 * 32], prod[:, 2 * BLK : 3 * BLK].rearrange("p (v d) -> p v d", d=D), AX.X, ALU.add)
        nc.vector.scalar_tensor_tensor(prod[:, 3 * BLK : 4 * BLK], c2[:, 3 * BLK : 4 * BLK], 1.0 / D, hf3[:], ALU.add, ALU.mult)
        nc.vector.tensor_reduce(res[:, 3 * 32 : 4 * 32], prod[:, 3 * BLK : 4 * BLK].rearrange("p (v d) -> p v d", d=D), AX.X, ALU.add)
        nc.sync.dma_start(out=out[:, 0:128], in_=res[:, 0:128])
